import numpy as np
import ml_dtypes


def mxq(x, axis, fmt="e4m3"):
    dtype, down = {"e4m3": (ml_dtypes.float8_e4m3fn, 7), "e5m2": (ml_dtypes.float8_e5m2, 14)}[fmt]
    v = np.moveaxis(np.asarray(x, np.float32).astype(ml_dtypes.bfloat16).astype(np.float64), axis, -1)
    blocks = v.reshape(v.shape[:-1] + (-1, 32))
    amax = np.abs(blocks).max(-1, keepdims=True)
    byte = np.maximum(np.where(amax > 0, np.frexp(amax)[1] - 1 + 127, 0) - down, 1)
    scale = np.exp2(byte - 127.0)
    codes = (blocks / scale).astype(np.float32).astype(dtype).astype(np.float64)
    return np.moveaxis((codes * scale).reshape(v.shape), -1, axis)


WIDE = False


def mx_kscale(k, group=512):
    if not WIDE:
        return np.ones(k)
    levels = np.array([18, -18])
    if group != 512:
        return np.exp2(np.random.permutation(np.resize(levels, k // group))).repeat(group)
    if k % 512:
        return np.exp2(np.random.permutation(np.resize(levels, k // 32))).repeat(32)
    a = np.empty((k // 512, 16))
    for p in range(k // 512):
        a[p, :8] = np.random.permutation(np.resize(levels, 8))
        for g in range(8):
            far = levels[np.abs(levels - a[p, g]) >= 10]
            a[p, g + 8] = far[np.random.randint(len(far))]
    return np.exp2(a.ravel()).repeat(32)


def f64(x):
    return np.asarray(x).astype(np.float64)


G, D, M, O, N = 4, 128, 128, 128, 512


def sgn(shape):
    return np.random.uniform(0.5, 2.0, shape) * np.where(np.random.standard_normal(shape) < 0, -1.0, 1.0)


def setup_inputs():
    n = np.random.standard_normal
    s_d = mx_kscale(D, 0)
    s_m = mx_kscale(M, 0)
    return {
        "x": (n((G, D, N)) * s_d[:, None]).astype(np.float32),
        "w1": (n((G, D, M)) / np.sqrt(D) / s_d[:, None]).astype(np.float32),
        "w2": (n((G, D, M)) / np.sqrt(D) / s_d[:, None]).astype(np.float32),
        "hs": (sgn((G, M, 1)) * s_m[:, None]).astype(np.float32),
        "wo2": (n((G, M, O)) / np.sqrt(M) / s_m[:, None]).astype(np.float32),
        "res": (0.5 * n((G, O, N))).astype(np.float32),
    }


def reference(x, w1, w2, hs, wo2, res):
    w1q = mxq(f64(w1), 1, "e4m3")
    xq = mxq(f64(x), 1, "e4m3")
    z1 = w1q.transpose(0, 2, 1) @ xq
    w2q = mxq(f64(w2), 1, "e4m3")
    z2 = w2q.transpose(0, 2, 1) @ xq
    pr = z1 * z2
    mu = np.mean(pr, axis=-1, keepdims=True)
    ms = np.sqrt(np.mean(np.square(z1), axis=-1, keepdims=True) + 0.1)
    h = (pr - mu) / ms
    hh = h * f64(hs)
    wo2q = mxq(f64(wo2), 1, "e4m3")
    hhq = mxq(hh, 1, "e4m3")
    y0 = wo2q.transpose(0, 2, 1) @ hhq
    y = y0 + f64(res)
    return y

@@ -1,0 +1,174 @@
+from contextlib import ExitStack
+
+import concourse.mybir as mybir
+
+G, D, M, O, N = 4, 128, 128, 128, 512
+FLOPS = 3 * 2 * G * D * M * N
+
+F32 = mybir.dt.float32
+BF16 = mybir.dt.bfloat16
+U32 = mybir.dt.uint32
+U8 = mybir.dt.uint8
+FP8X4 = mybir.dt.float8_e4m3fn_x4
+ALU = mybir.AluOpType
+ACT = mybir.ActivationFunctionType
+
+P = 128
+PACK = 4
+ROWS = 32
+HALF = N // 2
+RUN = 4
+EPS = 0.1
+X_SPLIT = 176
+H_SPLIT = 336
+
+
+def interleave(copy, dst, src, c0, c1):
+    copy(
+        out=dst[:, c0:c1, :].rearrange("p (c i) t -> p c t i", i=RUN),
+        in_=src[:, :, c0:c1].rearrange("p t (c i) -> p c t i", i=RUN),
+    )
+
+
+def tile_rows_frowcorr_kernel(tc, x, w1, w2, hs, wo2, res, out):
+    nc = tc.nc
+    with ExitStack() as ctx:
+        sb = ctx.enter_context(tc.tile_pool(name="sb", bufs=1))
+        ps = ctx.enter_context(tc.psum_pool(name="ps", bufs=1))
+        ctx.enter_context(tc.manual_schedule())
+
+        def tile(name, shape, dtype):
+            return sb.tile(shape, dtype, name=name, align_bytes=64)
+
+        def packed(t):
+            return t.rearrange("g (p j) c -> (g p) j c", j=PACK)
+
+        def quantize(codes, scales, words):
+            nc.vector.quantize_mx(
+                out=codes.bitcast(FP8X4), scales=scales, in_=words.rearrange("p c t -> p (c t)")
+            )
+
+        def products(banks, w_codes, w_scales, a_codes, a_scales):
+            for g in range(G):
+                rows = slice(ROWS * g, ROWS * (g + 1))
+                nc.tensor.matmul_mx(
+                    out=banks[g][:],
+                    lhsT=w_codes[rows, :].bitcast(FP8X4),
+                    lhsT_scale=w_scales[rows, :],
+                    rhs=a_codes[rows, :].bitcast(FP8X4),
+                    rhs_scale=a_scales[rows, :],
+                    start=True,
+                    stop=True,
+                )
+
+        raw, words, codes, scales = {}, {}, {}, {}
+        for name in ("w1", "w2", "wo2"):
+            raw[name] = tile(name + "_raw", [P, PACK, M], F32)
+            words[name] = tile(name + "_words", [P, M, PACK], BF16)
+            codes[name] = tile(name + "_codes", [P, M], U32)
+            scales[name] = tile(name + "_scales", [P, M], U8)
+        x_raw = [tile("x_raw%d" % h, [P, PACK, HALF], F32) for h in range(2)]
+        x_words = [tile("x_words%d" % h, [P, HALF, PACK], BF16) for h in range(2)]
+        x_codes = tile("x_codes", [P, N], U32)
+        x_scales = tile("x_scales", [P, N], U8)
+        hs_rows = tile("hs_rows", [P, G * ROWS], F32)
+        hs_cols = tile("hs_cols", [P, G * ROWS], F32)
+        res_sb = tile("res_sb", [P, G, N], F32)
+        z1s = [tile("z1s%d" % g, [P, N], F32) for g in range(G)]
+        sq = [tile("sq%d" % g, [P, N], BF16) for g in range(G)]
+        pr = [tile("pr%d" % g, [P, N], F32) for g in range(G)]
+        hh = [tile("hh%d" % g, [P, N], BF16) for g in range(G)]
+        y = [tile("y%d" % g, [P, N], F32) for g in range(G)]
+        sq_sum = tile("sq_sum", [P, G], F32)
+        rstd = tile("rstd", [P, G], F32)
+        pr_sum = tile("pr_sum", [P, G], F32)
+        mu = tile("mu", [P, G], F32)
+        h_rows = tile("h_rows", [P, PACK, N], BF16)
+        h_words = tile("h_words", [P, N, PACK], BF16)
+        h_codes = tile("h_codes", [P, N], U32)
+        h_scales = tile("h_scales", [P, N], U8)
+        bank_a = [ps.tile([P, N], F32, name="bank_a%d" % g) for g in range(G)]
+        bank_b = [ps.tile([P, N], F32, name="bank_b%d" % g) for g in range(G)]
+
+        nc.vector.memset(hs_rows[:], 0.0)
+        nc.sync.dma_start(out=raw["w1"][:], in_=packed(w1))
+        nc.scalar.dma_start(
+            out=hs_rows[0:P:ROWS, :].rearrange("a (g i) -> a g i", g=G),
+            in_=hs.rearrange("g (a i) o -> a g (i o)", i=ROWS),
+        )
+        for h in range(2):
+            nc.sync.dma_start(out=x_raw[h][:], in_=packed(x)[:, :, h * HALF : (h + 1) * HALF])
+        nc.sync.dma_start(out=raw["w2"][:], in_=packed(w2))
+        nc.sync.dma_start(out=raw["wo2"][:], in_=packed(wo2))
+        nc.sync.dma_start(out=res_sb[:], in_=res.rearrange("g o n -> o g n"))
+
+        interleave(nc.vector.tensor_copy, words["w1"], raw["w1"], 0, M)
+        nc.vector.transpose(out=hs_cols[:], in_=hs_rows[:])
+        quantize(codes["w1"][:], scales["w1"][:], words["w1"][:])
+        for h in range(2):
+            interleave(nc.vector.tensor_copy, x_words[h], x_raw[h], 0, X_SPLIT)
+            interleave(nc.scalar.copy, x_words[h], x_raw[h], X_SPLIT, HALF)
+            cols = slice(h * HALF, (h + 1) * HALF)
+            quantize(x_codes[:, cols], x_scales[:, cols], x_words[h][:])
+        products(bank_a, codes["w1"], scales["w1"], x_codes, x_scales)
+        interleave(nc.scalar.copy, words["w2"], raw["w2"], 0, M)
+        quantize(codes["w2"][:], scales["w2"][:], words["w2"][:])
+        products(bank_b, codes["w2"], scales["w2"], x_codes, x_scales)
+
+        def col(t, g):
+            return t[:, g : g + 1]
+
+        def scaled_copy(g):
+            nc.scalar.activation(
+                out=z1s[g][:], in_=bank_a[g][:], func=ACT.Copy, scale=hs_cols[:, ROWS * g : ROWS * g + 1]
+            )
+
+        def squares(g):
+            nc.scalar.activation(out=sq[g][:], in_=bank_a[g][:], func=ACT.Square, accum_out=col(sq_sum, g))
+
+        def root(g):
+            nc.scalar.activation(
+                out=col(rstd, g), in_=col(sq_sum, g), func=ACT.Abs_reciprocal_sqrt, scale=1.0 / N, bias=EPS
+            )
+
+        def product(g):
+            nc.vector.scalar_tensor_tensor(
+                out=pr[g][:], in0=bank_b[g][:], scalar=1.0, in1=z1s[g][:],
+                op0=ALU.mult, op1=ALU.mult, accum_out=col(pr_sum, g),
+            )
+
+        def mean(g):
+            nc.vector.tensor_scalar(
+                out=col(mu, g), in0=col(pr_sum, g), scalar1=1.0 / N, scalar2=None, op0=ALU.mult
+            )
+
+        def finish(g):
+            nc.vector.tensor_scalar(
+                out=hh[g][:], in0=pr[g][:], scalar1=col(mu, g), scalar2=col(rstd, g),
+                op0=ALU.subtract, op1=ALU.mult,
+            )
+            nc.sync.dma_start(out=h_rows[ROWS * g : ROWS * (g + 1), :, :], in_=hh[g][:])
+
+        scaled_copy(0)
+        for g in range(G):
+            if g + 1 < G:
+                scaled_copy(g + 1)
+            product(g)
+            if g > 0:
+                root(g - 1)
+            squares(g)
+            if g > 0:
+                finish(g - 1)
+            mean(g)
+        root(G - 1)
+        finish(G - 1)
+
+        interleave(nc.scalar.copy, words["wo2"], raw["wo2"], 0, O)
+        quantize(codes["wo2"][:], scales["wo2"][:], words["wo2"][:])
+        interleave(nc.vector.tensor_copy, h_words, h_rows, 0, H_SPLIT)
+        interleave(nc.scalar.copy, h_words, h_rows, H_SPLIT, N)
+        quantize(h_codes[:], h_scales[:], h_words[:])
+        products(bank_a, codes["wo2"], scales["wo2"], h_codes, h_scales)
+        for g in range(G):
+            nc.vector.tensor_tensor(out=y[g][:], in0=bank_a[g][:], in1=res_sb[:, g, :], op=ALU.add)
+            nc.sync.dma_start(out=out[g], in_=y[g][:])

@@ -48,8 +48,8 @@ def tile_rows_frowcorr_kernel(tc, x, w1, w2, hs, wo2, res, out):
                 out=codes.bitcast(FP8X4), scales=scales, in_=words.rearrange("p c t -> p (c t)")
             )
 
-        def products(banks, w_codes, w_scales, a_codes, a_scales):
-            for g in range(G):
+        def products(groups, banks, w_codes, w_scales, a_codes, a_scales):
+            for g in groups:
                 rows = slice(ROWS * g, ROWS * (g + 1))
                 nc.tensor.matmul_mx(
                     out=banks[g][:],
@@ -85,43 +85,42 @@ def tile_rows_frowcorr_kernel(tc, x, w1, w2, hs, wo2, res, out):
         mu = tile("mu", [P, G], F32)
         h_rows = tile("h_rows", [P, PACK, N], BF16)
         h_words = tile("h_words", [P, N, PACK], BF16)
-        h_codes = tile("h_codes", [P, N], U32)
-        h_scales = tile("h_scales", [P, N], U8)
+        h_codes = [tile("h_codes%d" % k, [P, N], U32) for k in range(2)]
+        h_scales = [tile("h_scales%d" % k, [P, N], U8) for k in range(2)]
+        one = tile("one", [P, 1], F32)
+        preload = tile("preload", [P, 1], F32)
         bank_a = [ps.tile([P, N], F32, name="bank_a%d" % g) for g in range(G)]
         bank_b = [ps.tile([P, N], F32, name="bank_b%d" % g) for g in range(G)]
 
         nc.vector.memset(hs_rows[:], 0.0)
+        nc.vector.memset(one[:], 1.0)
+        nc.scalar.activation(out=preload[:], in_=one[:], func=ACT.Abs_reciprocal_sqrt)
         nc.sync.dma_start(out=raw["w1"][:], in_=packed(w1))
-        nc.scalar.dma_start(
+        nc.sync.dma_start(out=x_raw[0][:], in_=packed(x)[:, :, 0:HALF])
+        nc.sync.dma_start(
             out=hs_rows[0:P:ROWS, :].rearrange("a (g i) -> a g i", g=G),
             in_=hs.rearrange("g (a i) o -> a g (i o)", i=ROWS),
         )
-        for h in range(2):
-            nc.sync.dma_start(out=x_raw[h][:], in_=packed(x)[:, :, h * HALF : (h + 1) * HALF])
+        nc.sync.dma_start(out=x_raw[1][:], in_=packed(x)[:, :, HALF:N])
         nc.sync.dma_start(out=raw["w2"][:], in_=packed(w2))
         nc.sync.dma_start(out=raw["wo2"][:], in_=packed(wo2))
         nc.sync.dma_start(out=res_sb[:], in_=res.rearrange("g o n -> o g n"))
 
         interleave(nc.vector.tensor_copy, words["w1"], raw["w1"], 0, M)
-        nc.vector.transpose(out=hs_cols[:], in_=hs_rows[:])
         quantize(codes["w1"][:], scales["w1"][:], words["w1"][:])
         for h in range(2):
             interleave(nc.vector.tensor_copy, x_words[h], x_raw[h], 0, X_SPLIT)
             interleave(nc.scalar.copy, x_words[h], x_raw[h], X_SPLIT, HALF)
             cols = slice(h * HALF, (h + 1) * HALF)
             quantize(x_codes[:, cols], x_scales[:, cols], x_words[h][:])
-        products(bank_a, codes["w1"], scales["w1"], x_codes, x_scales)
+        products(range(G), bank_a, codes["w1"], scales["w1"], x_codes, x_scales)
+        nc.vector.transpose(out=hs_cols[:], in_=hs_rows[:])
         interleave(nc.scalar.copy, words["w2"], raw["w2"], 0, M)
         quantize(codes["w2"][:], scales["w2"][:], words["w2"][:])
-        products(bank_b, codes["w2"], scales["w2"], x_codes, x_scales)
+        products(range(G), bank_b, codes["w2"], scales["w2"], x_codes, x_scales)
 
         def col(t, g):
             return t[:, g : g + 1]
-
-        def scaled_copy(g):
-            nc.scalar.activation(
-                out=z1s[g][:], in_=bank_a[g][:], func=ACT.Copy, scale=hs_cols[:, ROWS * g : ROWS * g + 1]
-            )
 
         def squares(g):
             nc.scalar.activation(out=sq[g][:], in_=bank_a[g][:], func=ACT.Square, accum_out=col(sq_sum, g))
@@ -133,13 +132,13 @@ def tile_rows_frowcorr_kernel(tc, x, w1, w2, hs, wo2, res, out):
 
         def product(g):
             nc.vector.scalar_tensor_tensor(
-                out=pr[g][:], in0=bank_b[g][:], scalar=1.0, in1=z1s[g][:],
+                out=pr[g][:], in0=bank_b[g][:], scalar=hs_cols[:, ROWS * g : ROWS * g + 1], in1=z1s[g][:],
                 op0=ALU.mult, op1=ALU.mult, accum_out=col(pr_sum, g),
             )
 
-        def mean(g):
+        def means(g0, g1):
             nc.vector.tensor_scalar(
-                out=col(mu, g), in0=col(pr_sum, g), scalar1=1.0 / N, scalar2=None, op0=ALU.mult
+                out=mu[:, g0:g1], in0=pr_sum[:, g0:g1], scalar1=1.0 / N, scalar2=None, op0=ALU.mult
             )
 
         def finish(g):
@@ -149,26 +148,46 @@ def tile_rows_frowcorr_kernel(tc, x, w1, w2, hs, wo2, res, out):
             )
             nc.sync.dma_start(out=h_rows[ROWS * g : ROWS * (g + 1), :, :], in_=hh[g][:])
 
-        scaled_copy(0)
-        for g in range(G):
-            if g + 1 < G:
-                scaled_copy(g + 1)
-            product(g)
-            if g > 0:
-                root(g - 1)
-            squares(g)
-            if g > 0:
-                finish(g - 1)
-            mean(g)
-        root(G - 1)
-        finish(G - 1)
+        nc.scalar.copy(out=z1s[0][:], in_=bank_a[0][:])
+        nc.vector.tensor_copy(out=z1s[1][:], in_=bank_a[1][:])
+        squares(0)
+        squares(1)
+        root(0)
+        nc.scalar.copy(out=z1s[2][:], in_=bank_a[2][:])
+        root(1)
+        nc.scalar.copy(out=z1s[3][:], in_=bank_a[3][:])
+        squares(2)
+        squares(3)
+        root(2)
+        root(3)
+        product(0)
+        product(1)
+        means(0, 2)
+        finish(0)
+        finish(1)
+        product(2)
+        product(3)
+        means(2, 4)
+        finish(2)
+        finish(3)
 
-        interleave(nc.scalar.copy, words["wo2"], raw["wo2"], 0, O)
-        quantize(codes["wo2"][:], scales["wo2"][:], words["wo2"][:])
-        interleave(nc.vector.tensor_copy, h_words, h_rows, 0, H_SPLIT)
-        interleave(nc.scalar.copy, h_words, h_rows, H_SPLIT, N)
-        quantize(h_codes[:], h_scales[:], h_words[:])
-        products(bank_a, codes["wo2"], scales["wo2"], h_codes, h_scales)
-        for g in range(G):
+        def words_of(first):
+            rows = slice(ROWS * first, ROWS * (first + 2))
+            interleave(nc.vector.tensor_copy, h_words[rows], h_rows[rows], 0, H_SPLIT)
+            interleave(nc.scalar.copy, h_words[rows], h_rows[rows], H_SPLIT, N)
+
+        def add_and_store(g):
             nc.vector.tensor_tensor(out=y[g][:], in0=bank_a[g][:], in1=res_sb[:, g, :], op=ALU.add)
             nc.sync.dma_start(out=out[g], in_=y[g][:])
+
+        interleave(nc.scalar.copy, words["wo2"], raw["wo2"], 0, O)
+        words_of(0)
+        quantize(codes["wo2"][:], scales["wo2"][:], words["wo2"][:])
+        quantize(h_codes[0][0 : 2 * ROWS], h_scales[0][0 : 2 * ROWS], h_words[0 : 2 * ROWS])
+        products(range(0, 2), bank_a, codes["wo2"], scales["wo2"], h_codes[0], h_scales[0])
+        words_of(2)
+        add_and_store(0)
+        quantize(h_codes[1][:], h_scales[1][:], h_words[:])
+        products(range(2, 4), bank_a, codes["wo2"], scales["wo2"], h_codes[1], h_scales[1])
+        for g in range(1, G):
+            add_and_store(g)

@@ -17,10 +17,11 @@ P = 128
 PACK = 4
 ROWS = 32
 HALF = N // 2
+PASS = 128
 RUN = 4
 EPS = 0.1
 X_SPLIT = 176
-H_SPLIT = 336
+H_SPLIT = (112, 128)
 
 
 def interleave(copy, dst, src, c0, c1):
@@ -48,18 +49,8 @@ def tile_rows_frowcorr_kernel(tc, x, w1, w2, hs, wo2, res, out):
                 out=codes.bitcast(FP8X4), scales=scales, in_=words.rearrange("p c t -> p (c t)")
             )
 
-        def products(groups, banks, w_codes, w_scales, a_codes, a_scales):
-            for g in groups:
-                rows = slice(ROWS * g, ROWS * (g + 1))
-                nc.tensor.matmul_mx(
-                    out=banks[g][:],
-                    lhsT=w_codes[rows, :].bitcast(FP8X4),
-                    lhsT_scale=w_scales[rows, :],
-                    rhs=a_codes[rows, :].bitcast(FP8X4),
-                    rhs_scale=a_scales[rows, :],
-                    start=True,
-                    stop=True,
-                )
+        def half(h):
+            return slice(h * HALF, (h + 1) * HALF)
 
         raw, words, codes, scales = {}, {}, {}, {}
         for name in ("w1", "w2", "wo2"):
@@ -69,8 +60,8 @@ def tile_rows_frowcorr_kernel(tc, x, w1, w2, hs, wo2, res, out):
             scales[name] = tile(name + "_scales", [P, M], U8)
         x_raw = [tile("x_raw%d" % h, [P, PACK, HALF], F32) for h in range(2)]
         x_words = [tile("x_words%d" % h, [P, HALF, PACK], BF16) for h in range(2)]
-        x_codes = tile("x_codes", [P, N], U32)
-        x_scales = tile("x_scales", [P, N], U8)
+        x_codes = [tile("x_codes%d" % h, [P, HALF], U32) for h in range(2)]
+        x_scales = [tile("x_scales%d" % h, [P, HALF], U8) for h in range(2)]
         hs_rows = tile("hs_rows", [P, G * ROWS], F32)
         hs_cols = tile("hs_cols", [P, G * ROWS], F32)
         res_sb = tile("res_sb", [P, G, N], F32)
@@ -83,25 +74,38 @@ def tile_rows_frowcorr_kernel(tc, x, w1, w2, hs, wo2, res, out):
         rstd = tile("rstd", [P, G], F32)
         pr_sum = tile("pr_sum", [P, G], F32)
         mu = tile("mu", [P, G], F32)
-        h_rows = tile("h_rows", [P, PACK, N], BF16)
-        h_words = tile("h_words", [P, N, PACK], BF16)
-        h_codes = [tile("h_codes%d" % k, [P, N], U32) for k in range(2)]
-        h_scales = [tile("h_scales%d" % k, [P, N], U8) for k in range(2)]
+        h_rows = [tile("h_rows%d" % h, [P, PACK, HALF], BF16) for h in range(2)]
+        h_words = [tile("h_words%d" % h, [P, HALF, PACK], BF16) for h in range(2)]
+        h_codes = [[tile("h_codes%d%d" % (k, h), [P, HALF], U32) for h in range(2)] for k in range(2)]
+        h_scales = [[tile("h_scales%d%d" % (k, h), [P, HALF], U8) for h in range(2)] for k in range(2)]
         one = tile("one", [P, 1], F32)
         preload = tile("preload", [P, 1], F32)
         bank_a = [ps.tile([P, N], F32, name="bank_a%d" % g) for g in range(G)]
         bank_b = [ps.tile([P, N], F32, name="bank_b%d" % g) for g in range(G)]
 
+        def matmuls(g, dst, name, a_codes, a_scales, starts=range(0, HALF, PASS)):
+            rows = slice(ROWS * g, ROWS * (g + 1))
+            for c in starts:
+                nc.tensor.matmul_mx(
+                    out=dst[:, c : c + PASS],
+                    lhsT=codes[name][rows, :].bitcast(FP8X4),
+                    lhsT_scale=scales[name][rows, :],
+                    rhs=a_codes[rows, c : c + PASS].bitcast(FP8X4),
+                    rhs_scale=a_scales[rows, c : c + PASS],
+                    start=True,
+                    stop=True,
+                )
+
         nc.vector.memset(hs_rows[:], 0.0)
         nc.vector.memset(one[:], 1.0)
         nc.scalar.activation(out=preload[:], in_=one[:], func=ACT.Abs_reciprocal_sqrt)
         nc.sync.dma_start(out=raw["w1"][:], in_=packed(w1))
-        nc.sync.dma_start(out=x_raw[0][:], in_=packed(x)[:, :, 0:HALF])
+        nc.sync.dma_start(out=x_raw[0][:], in_=packed(x)[:, :, half(0)])
         nc.sync.dma_start(
             out=hs_rows[0:P:ROWS, :].rearrange("a (g i) -> a g i", g=G),
             in_=hs.rearrange("g (a i) o -> a g (i o)", i=ROWS),
         )
-        nc.sync.dma_start(out=x_raw[1][:], in_=packed(x)[:, :, HALF:N])
+        nc.sync.dma_start(out=x_raw[1][:], in_=packed(x)[:, :, half(1)])
         nc.sync.dma_start(out=raw["w2"][:], in_=packed(w2))
         nc.sync.dma_start(out=raw["wo2"][:], in_=packed(wo2))
         nc.sync.dma_start(out=res_sb[:], in_=res.rearrange("g o n -> o g n"))
@@ -111,13 +115,27 @@ def tile_rows_frowcorr_kernel(tc, x, w1, w2, hs, wo2, res, out):
         for h in range(2):
             interleave(nc.vector.tensor_copy, x_words[h], x_raw[h], 0, X_SPLIT)
             interleave(nc.scalar.copy, x_words[h], x_raw[h], X_SPLIT, HALF)
-            cols = slice(h * HALF, (h + 1) * HALF)
-            quantize(x_codes[:, cols], x_scales[:, cols], x_words[h][:])
-        products(range(G), bank_a, codes["w1"], scales["w1"], x_codes, x_scales)
-        nc.vector.transpose(out=hs_cols[:], in_=hs_rows[:])
+            if h == 1:
+                nc.vector.transpose(out=hs_cols[:], in_=hs_rows[:])
+            quantize(x_codes[h][:], x_scales[h][:], x_words[h][:])
         interleave(nc.scalar.copy, words["w2"], raw["w2"], 0, M)
         quantize(codes["w2"][:], scales["w2"][:], words["w2"][:])
-        products(range(G), bank_b, codes["w2"], scales["w2"], x_codes, x_scales)
+        interleave(nc.vector.tensor_copy, words["wo2"], raw["wo2"], 0, O)
+
+        def z1_half(g, h):
+            matmuls(g, bank_a[g][:, half(h)], "w1", x_codes[h], x_scales[h])
+
+        def z2_whole(g):
+            for h in range(2):
+                matmuls(g, bank_b[g][:, half(h)], "w2", x_codes[h], x_scales[h])
+
+        for g in range(G):
+            z1_half(g, 0)
+        for pair in ((0, 1), (2, 3)):
+            for g in pair:
+                z1_half(g, 1)
+            for g in pair:
+                z2_whole(g)
 
         def col(t, g):
             return t[:, g : g + 1]
@@ -125,69 +143,63 @@ def tile_rows_frowcorr_kernel(tc, x, w1, w2, hs, wo2, res, out):
         def squares(g):
             nc.scalar.activation(out=sq[g][:], in_=bank_a[g][:], func=ACT.Square, accum_out=col(sq_sum, g))
 
-        def root(g):
-            nc.scalar.activation(
-                out=col(rstd, g), in_=col(sq_sum, g), func=ACT.Abs_reciprocal_sqrt, scale=1.0 / N, bias=EPS
-            )
-
         def product(g):
             nc.vector.scalar_tensor_tensor(
                 out=pr[g][:], in0=bank_b[g][:], scalar=hs_cols[:, ROWS * g : ROWS * g + 1], in1=z1s[g][:],
                 op0=ALU.mult, op1=ALU.mult, accum_out=col(pr_sum, g),
             )
 
-        def means(g0, g1):
-            nc.vector.tensor_scalar(
-                out=mu[:, g0:g1], in0=pr_sum[:, g0:g1], scalar1=1.0 / N, scalar2=None, op0=ALU.mult
+        def first_layer(pair):
+            cols = slice(pair[0], pair[1] + 1)
+            for g in pair:
+                squares(g)
+            nc.scalar.activation(
+                out=rstd[:, cols], in_=sq_sum[:, cols], func=ACT.Abs_reciprocal_sqrt, scale=1.0 / N, bias=EPS
             )
+            for g in pair:
+                product(g)
 
-        def finish(g):
-            nc.vector.tensor_scalar(
-                out=hh[g][:], in0=pr[g][:], scalar1=col(mu, g), scalar2=col(rstd, g),
-                op0=ALU.subtract, op1=ALU.mult,
-            )
-            nc.sync.dma_start(out=h_rows[ROWS * g : ROWS * (g + 1), :, :], in_=hh[g][:])
+        def finish(pair):
+            for g in pair:
+                nc.vector.tensor_scalar(
+                    out=col(mu, g), in0=col(pr_sum, g), scalar1=1.0 / N, scalar2=None, op0=ALU.mult
+                )
+            for h in range(2):
+                for g in pair:
+                    nc.vector.tensor_scalar(
+                        out=hh[g][:, half(h)], in0=pr[g][:, half(h)], scalar1=col(mu, g), scalar2=col(rstd, g),
+                        op0=ALU.subtract, op1=ALU.mult,
+                    )
+                    nc.sync.dma_start(out=h_rows[h][ROWS * g : ROWS * (g + 1), :, :], in_=hh[g][:, half(h)])
+
+        def second_layer(k, pair):
+            rows = slice(ROWS * pair[0], ROWS * (pair[1] + 1))
+            upto = slice(0, rows.stop)
+            banks = (bank_a, bank_b)
+            for h in range(2):
+                interleave(nc.vector.tensor_copy, h_words[h][rows], h_rows[h][rows], 0, H_SPLIT[h])
+                interleave(nc.scalar.copy, h_words[h][rows], h_rows[h][rows], H_SPLIT[h], HALF)
+            for h in range(2):
+                for c in range(0, HALF, PASS):
+                    cols = slice(c, c + PASS)
+                    quantize(h_codes[k][h][upto, cols], h_scales[k][h][upto, cols], h_words[h][upto, cols])
+                    for g in pair:
+                        matmuls(g, banks[h][g][:, half(0)], "wo2", h_codes[k][h], h_scales[k][h], [c])
+            for h in range(2):
+                for g in pair:
+                    nc.vector.tensor_tensor(
+                        out=y[g][:, half(h)], in0=banks[h][g][:, half(0)], in1=res_sb[:, g, half(h)], op=ALU.add
+                    )
+                    nc.sync.dma_start(out=out[g, :, half(h)], in_=y[g][:, half(h)])
 
         nc.scalar.copy(out=z1s[0][:], in_=bank_a[0][:])
         nc.vector.tensor_copy(out=z1s[1][:], in_=bank_a[1][:])
-        squares(0)
-        squares(1)
-        root(0)
-        nc.scalar.copy(out=z1s[2][:], in_=bank_a[2][:])
-        root(1)
-        nc.scalar.copy(out=z1s[3][:], in_=bank_a[3][:])
-        squares(2)
-        squares(3)
-        root(2)
-        root(3)
-        product(0)
-        product(1)
-        means(0, 2)
-        finish(0)
-        finish(1)
-        product(2)
-        product(3)
-        means(2, 4)
-        finish(2)
-        finish(3)
-
-        def words_of(first):
-            rows = slice(ROWS * first, ROWS * (first + 2))
-            interleave(nc.vector.tensor_copy, h_words[rows], h_rows[rows], 0, H_SPLIT)
-            interleave(nc.scalar.copy, h_words[rows], h_rows[rows], H_SPLIT, N)
-
-        def add_and_store(g):
-            nc.vector.tensor_tensor(out=y[g][:], in0=bank_a[g][:], in1=res_sb[:, g, :], op=ALU.add)
-            nc.sync.dma_start(out=out[g], in_=y[g][:])
-
-        interleave(nc.scalar.copy, words["wo2"], raw["wo2"], 0, O)
-        words_of(0)
+        first_layer((0, 1))
         quantize(codes["wo2"][:], scales["wo2"][:], words["wo2"][:])
-        quantize(h_codes[0][0 : 2 * ROWS], h_scales[0][0 : 2 * ROWS], h_words[0 : 2 * ROWS])
-        products(range(0, 2), bank_a, codes["wo2"], scales["wo2"], h_codes[0], h_scales[0])
-        words_of(2)
-        add_and_store(0)
-        quantize(h_codes[1][:], h_scales[1][:], h_words[:])
-        products(range(2, 4), bank_a, codes["wo2"], scales["wo2"], h_codes[1], h_scales[1])
-        for g in range(1, G):
-            add_and_store(g)
+        finish((0, 1))
+        nc.scalar.copy(out=z1s[2][:], in_=bank_a[2][:])
+        nc.scalar.copy(out=z1s[3][:], in_=bank_a[3][:])
+        first_layer((2, 3))
+        finish((2, 3))
+        second_layer(0, (0, 1))
+        second_layer(1, (2, 3))

from contextlib import ExitStack

import concourse.mybir as mybir

G, D, M, O, N = 4, 128, 128, 128, 512
FLOPS = 3 * 2 * G * D * M * N

F32 = mybir.dt.float32
BF16 = mybir.dt.bfloat16
U32 = mybir.dt.uint32
U8 = mybir.dt.uint8
FP8X4 = mybir.dt.float8_e4m3fn_x4
ALU = mybir.AluOpType
ACT = mybir.ActivationFunctionType

P = 128
PACK = 4
ROWS = 32
HALF = N // 2
PASS = 128
RUN = 4
EPS = 0.1
X_SPLIT = 176
H_SPLIT = (112, 128)


def interleave(copy, dst, src, c0, c1):
    copy(
        out=dst[:, c0:c1, :].rearrange("p (c i) t -> p c t i", i=RUN),
        in_=src[:, :, c0:c1].rearrange("p t (c i) -> p c t i", i=RUN),
    )


def tile_rows_frowcorr_kernel(tc, x, w1, w2, hs, wo2, res, out):
    nc = tc.nc
    with ExitStack() as ctx:
        sb = ctx.enter_context(tc.tile_pool(name="sb", bufs=1))
        ps = ctx.enter_context(tc.psum_pool(name="ps", bufs=1))
        ctx.enter_context(tc.manual_schedule())

        def tile(name, shape, dtype):
            return sb.tile(shape, dtype, name=name, align_bytes=64)

        def packed(t):
            return t.rearrange("g (p j) c -> (g p) j c", j=PACK)

        def quantize(codes, scales, words):
            nc.vector.quantize_mx(
                out=codes.bitcast(FP8X4), scales=scales, in_=words.rearrange("p c t -> p (c t)")
            )

        def half(h):
            return slice(h * HALF, (h + 1) * HALF)

        raw, words, codes, scales = {}, {}, {}, {}
        for name in ("w1", "w2", "wo2"):
            raw[name] = tile(name + "_raw", [P, PACK, M], F32)
            words[name] = tile(name + "_words", [P, M, PACK], BF16)
            codes[name] = tile(name + "_codes", [P, M], U32)
            scales[name] = tile(name + "_scales", [P, M], U8)
        x_raw = [tile("x_raw%d" % h, [P, PACK, HALF], F32) for h in range(2)]
        x_words = [tile("x_words%d" % h, [P, HALF, PACK], BF16) for h in range(2)]
        x_codes = [tile("x_codes%d" % h, [P, HALF], U32) for h in range(2)]
        x_scales = [tile("x_scales%d" % h, [P, HALF], U8) for h in range(2)]
        hs_rows = tile("hs_rows", [P, G * ROWS], F32)
        hs_cols = tile("hs_cols", [P, G * ROWS], F32)
        res_sb = tile("res_sb", [P, G, N], F32)
        z1s = [tile("z1s%d" % g, [P, N], F32) for g in range(G)]
        sq = [tile("sq%d" % g, [P, N], BF16) for g in range(G)]
        pr = [tile("pr%d" % g, [P, N], F32) for g in range(G)]
        hh = [tile("hh%d" % g, [P, N], BF16) for g in range(G)]
        y = [tile("y%d" % g, [P, N], F32) for g in range(G)]
        sq_sum = tile("sq_sum", [P, G], F32)
        rstd = tile("rstd", [P, G], F32)
        pr_sum = tile("pr_sum", [P, G], F32)
        mu = tile("mu", [P, G], F32)
        h_rows = [tile("h_rows%d" % h, [P, PACK, HALF], BF16) for h in range(2)]
        h_words = [tile("h_words%d" % h, [P, HALF, PACK], BF16) for h in range(2)]
        h_codes = [[tile("h_codes%d%d" % (k, h), [P, HALF], U32) for h in range(2)] for k in range(2)]
        h_scales = [[tile("h_scales%d%d" % (k, h), [P, HALF], U8) for h in range(2)] for k in range(2)]
        one = tile("one", [P, 1], F32)
        preload = tile("preload", [P, 1], F32)
        bank_a = [ps.tile([P, N], F32, name="bank_a%d" % g) for g in range(G)]
        bank_b = [ps.tile([P, N], F32, name="bank_b%d" % g) for g in range(G)]

        def matmuls(g, dst, name, a_codes, a_scales, starts=range(0, HALF, PASS)):
            rows = slice(ROWS * g, ROWS * (g + 1))
            for c in starts:
                nc.tensor.matmul_mx(
                    out=dst[:, c : c + PASS],
                    lhsT=codes[name][rows, :].bitcast(FP8X4),
                    lhsT_scale=scales[name][rows, :],
                    rhs=a_codes[rows, c : c + PASS].bitcast(FP8X4),
                    rhs_scale=a_scales[rows, c : c + PASS],
                    start=True,
                    stop=True,
                )

        nc.vector.memset(hs_rows[:], 0.0)
        nc.vector.memset(one[:], 1.0)
        nc.scalar.activation(out=preload[:], in_=one[:], func=ACT.Abs_reciprocal_sqrt)
        nc.sync.dma_start(out=raw["w1"][:], in_=packed(w1))
        nc.sync.dma_start(out=x_raw[0][:], in_=packed(x)[:, :, half(0)])
        nc.sync.dma_start(
            out=hs_rows[0:P:ROWS, :].rearrange("a (g i) -> a g i", g=G),
            in_=hs.rearrange("g (a i) o -> a g (i o)", i=ROWS),
        )
        nc.sync.dma_start(out=x_raw[1][:], in_=packed(x)[:, :, half(1)])
        nc.sync.dma_start(out=raw["w2"][:], in_=packed(w2))
        nc.sync.dma_start(out=raw["wo2"][:], in_=packed(wo2))
        nc.sync.dma_start(out=res_sb[:], in_=res.rearrange("g o n -> o g n"))

        interleave(nc.vector.tensor_copy, words["w1"], raw["w1"], 0, M)
        quantize(codes["w1"][:], scales["w1"][:], words["w1"][:])
        for h in range(2):
            interleave(nc.vector.tensor_copy, x_words[h], x_raw[h], 0, X_SPLIT)
            interleave(nc.scalar.copy, x_words[h], x_raw[h], X_SPLIT, HALF)
            if h == 1:
                nc.vector.transpose(out=hs_cols[:], in_=hs_rows[:])
            quantize(x_codes[h][:], x_scales[h][:], x_words[h][:])
        interleave(nc.scalar.copy, words["w2"], raw["w2"], 0, M)
        quantize(codes["w2"][:], scales["w2"][:], words["w2"][:])
        interleave(nc.vector.tensor_copy, words["wo2"], raw["wo2"], 0, O)

        def z1_half(g, h):
            matmuls(g, bank_a[g][:, half(h)], "w1", x_codes[h], x_scales[h])

        def z2_whole(g):
            for h in range(2):
                matmuls(g, bank_b[g][:, half(h)], "w2", x_codes[h], x_scales[h])

        for g in range(G):
            z1_half(g, 0)
        for pair in ((0, 1), (2, 3)):
            for g in pair:
                z1_half(g, 1)
            for g in pair:
                z2_whole(g)

        def col(t, g):
            return t[:, g : g + 1]

        def squares(g):
            nc.scalar.activation(out=sq[g][:], in_=bank_a[g][:], func=ACT.Square, accum_out=col(sq_sum, g))

        def product(g):
            nc.vector.scalar_tensor_tensor(
                out=pr[g][:], in0=bank_b[g][:], scalar=hs_cols[:, ROWS * g : ROWS * g + 1], in1=z1s[g][:],
                op0=ALU.mult, op1=ALU.mult, accum_out=col(pr_sum, g),
            )

        def first_layer(pair):
            cols = slice(pair[0], pair[1] + 1)
            for g in pair:
                squares(g)
            nc.scalar.activation(
                out=rstd[:, cols], in_=sq_sum[:, cols], func=ACT.Abs_reciprocal_sqrt, scale=1.0 / N, bias=EPS
            )
            for g in pair:
                product(g)

        def finish(pair):
            for g in pair:
                nc.vector.tensor_scalar(
                    out=col(mu, g), in0=col(pr_sum, g), scalar1=1.0 / N, scalar2=None, op0=ALU.mult
                )
            for h in range(2):
                for g in pair:
                    nc.vector.tensor_scalar(
                        out=hh[g][:, half(h)], in0=pr[g][:, half(h)], scalar1=col(mu, g), scalar2=col(rstd, g),
                        op0=ALU.subtract, op1=ALU.mult,
                    )
                    nc.sync.dma_start(out=h_rows[h][ROWS * g : ROWS * (g + 1), :, :], in_=hh[g][:, half(h)])

        def second_layer(k, pair):
            rows = slice(ROWS * pair[0], ROWS * (pair[1] + 1))
            upto = slice(0, rows.stop)
            banks = (bank_a, bank_b)
            for h in range(2):
                interleave(nc.vector.tensor_copy, h_words[h][rows], h_rows[h][rows], 0, H_SPLIT[h])
                interleave(nc.scalar.copy, h_words[h][rows], h_rows[h][rows], H_SPLIT[h], HALF)
            for h in range(2):
                for c in range(0, HALF, PASS):
                    cols = slice(c, c + PASS)
                    quantize(h_codes[k][h][upto, cols], h_scales[k][h][upto, cols], h_words[h][upto, cols])
                    for g in pair:
                        matmuls(g, banks[h][g][:, half(0)], "wo2", h_codes[k][h], h_scales[k][h], [c])
            for h in range(2):
                for g in pair:
                    nc.vector.tensor_tensor(
                        out=y[g][:, half(h)], in0=banks[h][g][:, half(0)], in1=res_sb[:, g, half(h)], op=ALU.add
                    )
                    nc.sync.dma_start(out=out[g, :, half(h)], in_=y[g][:, half(h)])

        nc.scalar.copy(out=z1s[0][:], in_=bank_a[0][:])
        nc.vector.tensor_copy(out=z1s[1][:], in_=bank_a[1][:])
        first_layer((0, 1))
        quantize(codes["wo2"][:], scales["wo2"][:], words["wo2"][:])
        finish((0, 1))
        nc.scalar.copy(out=z1s[2][:], in_=bank_a[2][:])
        nc.scalar.copy(out=z1s[3][:], in_=bank_a[3][:])
        first_layer((2, 3))
        finish((2, 3))
        second_layer(0, (0, 1))
        second_layer(1, (2, 3))
